import numpy as np
import ml_dtypes


def mxq(x, axis, fmt="e4m3"):
    dtype, down = {"e4m3": (ml_dtypes.float8_e4m3fn, 7), "e5m2": (ml_dtypes.float8_e5m2, 14)}[fmt]
    v = np.moveaxis(np.asarray(x, np.float32).astype(ml_dtypes.bfloat16).astype(np.float64), axis, -1)
    blocks = v.reshape(v.shape[:-1] + (-1, 32))
    amax = np.abs(blocks).max(-1, keepdims=True)
    byte = np.maximum(np.where(amax > 0, np.frexp(amax)[1] - 1 + 127, 0) - down, 1)
    scale = np.exp2(byte - 127.0)
    codes = (blocks / scale).astype(np.float32).astype(dtype).astype(np.float64)
    return np.moveaxis((codes * scale).reshape(v.shape), -1, axis)


WIDE = False


def mx_kscale(k):
    if not WIDE:
        return np.ones(k)
    levels = np.array([10, -10, 5, -5, 0])
    if k % 512:
        return np.exp2(np.random.permutation(np.resize(levels, k // 32))).repeat(32)
    a = np.empty((k // 512, 16))
    for p in range(k // 512):
        a[p, :8] = np.random.permutation(np.resize(levels, 8))
        for g in range(8):
            far = levels[np.abs(levels - a[p, g]) >= 10]
            a[p, g + 8] = far[np.random.randint(len(far))]
    return np.exp2(a.ravel()).repeat(32)


def f64(x):
    return np.asarray(x).astype(np.float64)


def striped(idx):
    return np.tile(idx.reshape(-1, 16).T, (8, 1)).astype(np.uint16)


def unstriped(offs):
    return offs[:16].T.reshape(-1).astype(np.int64)


def pack_weight(w):
    k, n = w.shape
    w = f64(np.asarray(w, np.float32).astype(ml_dtypes.bfloat16)).reshape(k // 32, 32, n)
    amax = np.abs(w).max(1)
    byte = np.clip(np.where(amax > 0, np.frexp(amax)[1] - 1 + 127 - 7, 1), 1, 254)
    scaled = (w * np.exp2(127.0 - byte)[:, None, :]).reshape(k, n).astype(np.float32)
    words = np.ascontiguousarray(scaled.reshape(k // 512, 128, 4, n).transpose(0, 1, 3, 2)).astype(ml_dtypes.float8_e4m3fn).view(np.uint8)
    return words, np.ascontiguousarray(byte.astype(np.uint8).reshape(k // 512, 16, n))


def unpack_weight(words, scales):
    g, p, n, _ = words.shape
    vals = np.ascontiguousarray(words).view(ml_dtypes.float8_e4m3fn).astype(np.float64) * np.repeat(np.exp2(scales.astype(np.float64) - 127.0), 8, axis=1)[..., None]
    return vals.transpose(0, 1, 3, 2).reshape(g * 512, n)


K, T, S, N, U = 1024, 2048, 512, 256, 1024


def setup_inputs():
    n = np.random.standard_normal
    s = mx_kscale(K)[:, None]
    packed_w1 = pack_weight(n((K, N)) / np.sqrt(K) / s)
    return {
        "xT": (n((K, T)) * s).astype(np.float32),
        "mem": n((N, U)).astype(np.float32),
        "w1_words": packed_w1[0],
        "w1_scales": packed_w1[1],
        "offs": striped(np.random.permutation(T)[:S]),
        "slot": striped(np.random.permutation(U)[:S]),
    }


def reference(xT, mem, w1_words, w1_scales, offs, slot):
    xq = mxq(f64(xT)[:, unstriped(offs)], 0, "e4m3")
    y = np.tanh(unpack_weight(w1_words, w1_scales).T @ xq)
    out = f64(mem).copy()
    out[:, unstriped(slot)] = y
    return out

@@ -1,0 +1,94 @@
+from contextlib import ExitStack
+
+import concourse.mybir as mybir
+
+K, T, S, N, U = 1024, 2048, 512, 256, 1024
+FLOPS = 2 * K * N * S
+
+F32 = mybir.dt.float32
+BF16 = mybir.dt.bfloat16
+I32 = mybir.dt.int32
+U32 = mybir.dt.uint32
+U16 = mybir.dt.uint16
+U8 = mybir.dt.uint8
+FP8X4 = mybir.dt.float8_e4m3fn_x4
+TANH = mybir.ActivationFunctionType.Tanh
+
+P = 128
+PACK = 4
+PASSES = K // (P * PACK)
+BLOCKS = N // P
+HALVES = 2
+HALF = S // HALVES
+LANES = 16
+
+
+def tile_picked_kvput_tanh_e_kernel(tc, xT, mem, w1_words, w1_scales, offs, slot, out):
+    nc = tc.nc
+    with ExitStack() as ctx:
+        keep = ctx.enter_context(tc.tile_pool(name="keep", bufs=1))
+        psum = ctx.enter_context(tc.psum_pool(name="psum", bufs=1))
+
+        offs_sb = keep.tile([P, S // LANES], U16, name="offs_sb")
+        slot_sb = keep.tile([P, S // LANES], U16, name="slot_sb")
+        w_codes = keep.tile([P, PASSES, N], U32, name="w_codes", align_bytes=64)
+        w_scales = keep.tile([P, PASSES, N], U8, name="w_scales", align_bytes=64)
+        rows = [[keep.tile([P, T], F32, name=f"rows{z}{j}") for j in range(PACK)] for z in range(PASSES)]
+        store = [keep.tile([P, U], F32, name=f"store{b}") for b in range(BLOCKS)]
+
+        x_rows = xT.rearrange("(z p j) t -> z j p t", z=PASSES, j=PACK)
+        for z in range(PASSES):
+            for j in range(PACK):
+                nc.sync.dma_start(rows[z][j][:], x_rows[z, j])
+                if z == 0 and j == 0:
+                    nc.sync.dma_start(offs_sb[:], offs)
+        nc.sync.dma_start(w_codes[:].bitcast(I32), w1_words.rearrange("z p n r -> p z (n r)").bitcast(I32))
+        nc.sync.dma_start(slot_sb[:], slot)
+        for b in range(BLOCKS):
+            nc.sync.dma_start(store[b][:], mem[b * P : (b + 1) * P, :])
+
+        nc.gpsimd.memset(w_scales[:].rearrange("p z n -> p (z n)").bitcast(I32), 0)
+        for q in range(4):
+            nc.scalar.dma_start(
+                w_scales[32 * q : 32 * q + 4].bitcast(I32),
+                w1_scales[:, 4 * q : 4 * q + 4, :].rearrange("z r n -> r z n").bitcast(I32),
+            )
+
+        def entries(list_tile, h):
+            return list_tile[:, h * HALF // LANES : (h + 1) * HALF // LANES]
+
+        picked = [[keep.tile([P, HALF, PACK], BF16, name=f"picked{z}{h}", align_bytes=64) for h in range(HALVES)] for z in range(PASSES)]
+        x_codes = [[keep.tile([P, HALF], U32, name=f"x_codes{z}{h}", align_bytes=64) for h in range(HALVES)] for z in range(PASSES)]
+        x_scales = [[keep.tile([P, HALF], U8, name=f"x_scales{z}{h}", align_bytes=64) for h in range(HALVES)] for z in range(PASSES)]
+        for z in range(PASSES):
+            for j in range(PACK):
+                for h in range(HALVES):
+                    nc.vector.tensor_copy(picked[z][h][:, :, j], rows[z][j][:].indirect(entries(offs_sb, h)))
+                    if j == PACK - 1:
+                        nc.vector.quantize_mx(
+                            out=x_codes[z][h][:].bitcast(FP8X4),
+                            scales=x_scales[z][h][:],
+                            in_=picked[z][h][:].rearrange("p s j -> p (s j)"),
+                        )
+
+        y = {}
+        for h in range(HALVES):
+            for b in range(BLOCKS):
+                acc = psum.tile([P, HALF], F32, name=f"acc{h}{b}")
+                for z in range(PASSES):
+                    nc.tensor.matmul_mx(
+                        out=acc[:],
+                        lhsT=w_codes[:, z, b * P : (b + 1) * P].bitcast(FP8X4),
+                        lhsT_scale=w_scales[:, z, b * P : (b + 1) * P],
+                        rhs=x_codes[z][h][:].bitcast(FP8X4),
+                        rhs_scale=x_scales[z][h][:],
+                        start=(z == 0),
+                        stop=(z == PASSES - 1),
+                    )
+                y[h, b] = keep.tile([P, HALF], F32, name=f"y{h}{b}")
+                nc.scalar.activation(y[h, b][:], acc[:], TANH)
+
+        for b in range(BLOCKS):
+            for h in range(HALVES):
+                nc.vector.tensor_copy(store[b][:].indirect(entries(slot_sb, h)), y[h, b][:])
+            nc.sync.dma_start(out[b * P : (b + 1) * P, :], store[b][:])

@@ -33,62 +33,70 @@ def tile_picked_kvput_tanh_e_kernel(tc, xT, mem, w1_words, w1_scales, offs, slot
         slot_sb = keep.tile([P, S // LANES], U16, name="slot_sb")
         w_codes = keep.tile([P, PASSES, N], U32, name="w_codes", align_bytes=64)
         w_scales = keep.tile([P, PASSES, N], U8, name="w_scales", align_bytes=64)
-        rows = [[keep.tile([P, T], F32, name=f"rows{z}{j}") for j in range(PACK)] for z in range(PASSES)]
+        first_rows = keep.tile([P, 2, T], F32, name="first_rows")
+        rows = {(0, j): first_rows[:, j, :] for j in range(2)}
+        later = [(z, j) for z in range(PASSES) for j in range(PACK) if (z, j) not in rows]
+        for z, j in later:
+            rows[z, j] = keep.tile([P, T], F32, name=f"rows{z}{j}")[:]
         store = [keep.tile([P, U], F32, name=f"store{b}") for b in range(BLOCKS)]
 
-        x_rows = xT.rearrange("(z p j) t -> z j p t", z=PASSES, j=PACK)
-        for z in range(PASSES):
-            for j in range(PACK):
-                nc.sync.dma_start(rows[z][j][:], x_rows[z, j])
-                if z == 0 and j == 0:
-                    nc.sync.dma_start(offs_sb[:], offs)
-        nc.sync.dma_start(w_codes[:].bitcast(I32), w1_words.rearrange("z p n r -> p z (n r)").bitcast(I32))
+        nc.vector.memset(w_scales[:].rearrange("p z n -> p (z n)").bitcast(I32), 0)
+        x_rows = xT.rearrange("(z p j) t -> z p j t", z=PASSES, j=PACK)
+        nc.sync.dma_start(first_rows[:], x_rows[0, :, 0:2, :])
+        nc.sync.dma_start(offs_sb[:], offs)
         nc.sync.dma_start(slot_sb[:], slot)
-        for b in range(BLOCKS):
-            nc.sync.dma_start(store[b][:], mem[b * P : (b + 1) * P, :])
-
-        nc.gpsimd.memset(w_scales[:].rearrange("p z n -> p (z n)").bitcast(I32), 0)
+        for z, j in later:
+            nc.sync.dma_start(rows[z, j], x_rows[z, :, j, :])
         for q in range(4):
-            nc.scalar.dma_start(
+            nc.sync.dma_start(
                 w_scales[32 * q : 32 * q + 4].bitcast(I32),
                 w1_scales[:, 4 * q : 4 * q + 4, :].rearrange("z r n -> r z n").bitcast(I32),
             )
-
-        def entries(list_tile, h):
-            return list_tile[:, h * HALF // LANES : (h + 1) * HALF // LANES]
-
-        picked = [[keep.tile([P, HALF, PACK], BF16, name=f"picked{z}{h}", align_bytes=64) for h in range(HALVES)] for z in range(PASSES)]
-        x_codes = [[keep.tile([P, HALF], U32, name=f"x_codes{z}{h}", align_bytes=64) for h in range(HALVES)] for z in range(PASSES)]
-        x_scales = [[keep.tile([P, HALF], U8, name=f"x_scales{z}{h}", align_bytes=64) for h in range(HALVES)] for z in range(PASSES)]
-        for z in range(PASSES):
-            for j in range(PACK):
-                for h in range(HALVES):
-                    nc.vector.tensor_copy(picked[z][h][:, :, j], rows[z][j][:].indirect(entries(offs_sb, h)))
-                    if j == PACK - 1:
-                        nc.vector.quantize_mx(
-                            out=x_codes[z][h][:].bitcast(FP8X4),
-                            scales=x_scales[z][h][:],
-                            in_=picked[z][h][:].rearrange("p s j -> p (s j)"),
-                        )
-
-        y = {}
-        for h in range(HALVES):
-            for b in range(BLOCKS):
-                acc = psum.tile([P, HALF], F32, name=f"acc{h}{b}")
-                for z in range(PASSES):
-                    nc.tensor.matmul_mx(
-                        out=acc[:],
-                        lhsT=w_codes[:, z, b * P : (b + 1) * P].bitcast(FP8X4),
-                        lhsT_scale=w_scales[:, z, b * P : (b + 1) * P],
-                        rhs=x_codes[z][h][:].bitcast(FP8X4),
-                        rhs_scale=x_scales[z][h][:],
-                        start=(z == 0),
-                        stop=(z == PASSES - 1),
-                    )
-                y[h, b] = keep.tile([P, HALF], F32, name=f"y{h}{b}")
-                nc.scalar.activation(y[h, b][:], acc[:], TANH)
-
+        nc.sync.dma_start(w_codes[:].bitcast(I32), w1_words.rearrange("z p n r -> p z (n r)").bitcast(I32))
         for b in range(BLOCKS):
+            nc.sync.dma_start(store[b][:], mem[b * P : (b + 1) * P, :])
+
+        def entries(list_tile, lo, hi):
+            return list_tile[:, lo // LANES : hi // LANES]
+
+        x_codes = [keep.tile([P, S], U32, name=f"x_codes{z}", align_bytes=64) for z in range(PASSES)]
+        x_scales = [keep.tile([P, S], U8, name=f"x_scales{z}", align_bytes=64) for z in range(PASSES)]
+
+        def quantize(z, picked, base, lo, hi):
+            nc.vector.quantize_mx(
+                out=x_codes[z][:, lo:hi].bitcast(FP8X4),
+                scales=x_scales[z][:, lo:hi],
+                in_=picked[:, lo - base : hi - base, :].rearrange("p s j -> p (s j)"),
+            )
+
+        picked0 = keep.tile([P, S, PACK], BF16, name="picked0", align_bytes=64)
+        for j in range(PACK):
+            nc.vector.tensor_copy(picked0[:, :, j], rows[0, j].indirect(offs_sb[:]))
+        quantize(0, picked0, 0, 0, S)
+
+        picked1 = [keep.tile([P, HALF, PACK], BF16, name=f"picked1{h}", align_bytes=64) for h in range(HALVES)]
+        for j in range(PACK):
             for h in range(HALVES):
-                nc.vector.tensor_copy(store[b][:].indirect(entries(slot_sb, h)), y[h, b][:])
-            nc.sync.dma_start(out[b * P : (b + 1) * P, :], store[b][:])
+                nc.vector.tensor_copy(picked1[h][:, :, j], rows[1, j].indirect(entries(offs_sb, h * HALF, (h + 1) * HALF)))
+        for lo, hi in ((0, 128), (128, 256), (256, 512)):
+            quantize(1, picked1[lo // HALF], lo // HALF * HALF, lo, hi)
+
+        y = [keep.tile([P, S], F32, name=f"y{b}") for b in range(BLOCKS)]
+        for b, lo, hi in ((0, 0, 128), (1, 0, 256), (0, 128, 256), (0, 256, 512), (1, 256, 512)):
+            acc = psum.tile([P, hi - lo], F32, name="acc", bufs=3)
+            for z in range(PASSES):
+                nc.tensor.matmul_mx(
+                    out=acc[:],
+                    lhsT=w_codes[:, z, b * P : (b + 1) * P].bitcast(FP8X4),
+                    lhsT_scale=w_scales[:, z, b * P : (b + 1) * P],
+                    rhs=x_codes[z][:, lo:hi].bitcast(FP8X4),
+                    rhs_scale=x_scales[z][:, lo:hi],
+                    start=(z == 0),
+                    stop=(z == PASSES - 1),
+                )
+            nc.scalar.activation(y[b][:, lo:hi], acc[:], TANH)
+
+        for b, lo, hi in ((0, 0, 128), (1, 0, 256), (0, 128, 512), (1, 256, 512)):
+            nc.vector.tensor_copy(store[b][:].indirect(entries(slot_sb, lo, hi)), y[b][:, lo:hi])
+            if hi == S:
+                nc.sync.dma_start(out[b * P : (b + 1) * P, :], store[b][:])

@@ -13,6 +13,7 @@ U16 = mybir.dt.uint16
 U8 = mybir.dt.uint8
 FP8X4 = mybir.dt.float8_e4m3fn_x4
 TANH = mybir.ActivationFunctionType.Tanh
+COPY = mybir.ActivationFunctionType.Copy
 
 P = 128
 PACK = 4
@@ -21,6 +22,7 @@ BLOCKS = N // P
 HALVES = 2
 HALF = S // HALVES
 LANES = 16
+CUTS = (0, 768, 1280, 1792, 2048)
 
 
 def tile_picked_kvput_tanh_e_kernel(tc, xT, mem, w1_words, w1_scales, offs, slot, out):
@@ -35,9 +37,10 @@ def tile_picked_kvput_tanh_e_kernel(tc, xT, mem, w1_words, w1_scales, offs, slot
         w_scales = keep.tile([P, PASSES, N], U8, name="w_scales", align_bytes=64)
         first_rows = keep.tile([P, 2, T], F32, name="first_rows")
         rows = {(0, j): first_rows[:, j, :] for j in range(2)}
-        later = [(z, j) for z in range(PASSES) for j in range(PACK) if (z, j) not in rows]
+        later = [(0, 2), (0, 3), (1, 2), (1, 0), (1, 1), (1, 3)]
         for z, j in later:
             rows[z, j] = keep.tile([P, T], F32, name=f"rows{z}{j}")[:]
+        rounded = {j: keep.tile([P, T], BF16, name=f"rounded{j}") for j in (2, 3)}
         store = [keep.tile([P, U], F32, name=f"store{b}") for b in range(BLOCKS)]
 
         nc.vector.memset(w_scales[:].rearrange("p z n -> p (z n)").bitcast(I32), 0)
@@ -45,8 +48,10 @@ def tile_picked_kvput_tanh_e_kernel(tc, xT, mem, w1_words, w1_scales, offs, slot
         nc.sync.dma_start(first_rows[:], x_rows[0, :, 0:2, :])
         nc.sync.dma_start(offs_sb[:], offs)
         nc.sync.dma_start(slot_sb[:], slot)
-        for z, j in later:
+        for z, j in later[:-1]:
             nc.sync.dma_start(rows[z, j], x_rows[z, :, j, :])
+        for lo, hi in ((0, CUTS[2]), CUTS[2:4], CUTS[3:5]):
+            nc.sync.dma_start(rows[1, 3][:, lo:hi], x_rows[1, :, 3, lo:hi])
         for q in range(4):
             nc.sync.dma_start(
                 w_scales[32 * q : 32 * q + 4].bitcast(I32),
@@ -75,14 +80,28 @@ def tile_picked_kvput_tanh_e_kernel(tc, xT, mem, w1_words, w1_scales, offs, slot
         quantize(0, picked0, 0, 0, S)
 
         picked1 = [keep.tile([P, HALF, PACK], BF16, name=f"picked1{h}", align_bytes=64) for h in range(HALVES)]
-        for j in range(PACK):
+        half_list = [entries(offs_sb, h * HALF, (h + 1) * HALF) for h in range(HALVES)]
+
+        nc.scalar.activation(rounded[2][:], rows[1, 2], COPY)
+        nc.scalar.activation(picked1[1][:, :, 2], rounded[2][:].indirect(half_list[1]), COPY)
+        nc.vector.tensor_copy(picked1[0][:, :, 2], rows[1, 2].indirect(half_list[0]))
+        for j in range(2):
             for h in range(HALVES):
-                nc.vector.tensor_copy(picked1[h][:, :, j], rows[1, j].indirect(entries(offs_sb, h * HALF, (h + 1) * HALF)))
+                nc.vector.tensor_copy(picked1[h][:, :, j], rows[1, j].indirect(half_list[h]))
+        for n in range(4):
+            lo, hi = CUTS[n : n + 2]
+            if n % 2 == 0:
+                nc.vector.tensor_copy(rounded[3][:, lo:hi], rows[1, 3][:, lo:hi])
+            else:
+                nc.scalar.activation(rounded[3][:, lo:hi], rows[1, 3][:, lo:hi], COPY)
+        nc.vector.tensor_copy(picked1[0][:, :, 3], rows[1, 3].indirect(half_list[0]))
+        nc.scalar.activation(picked1[1][:, :, 3], rounded[3][:].indirect(half_list[1]), COPY)
         for lo, hi in ((0, 128), (128, 256), (256, 512)):
             quantize(1, picked1[lo // HALF], lo // HALF * HALF, lo, hi)
 
         y = [keep.tile([P, S], F32, name=f"y{b}") for b in range(BLOCKS)]
-        for b, lo, hi in ((0, 0, 128), (1, 0, 256), (0, 128, 256), (0, 256, 512), (1, 256, 512)):
+        pieces = ((0, 0, 128), (0, 128, 256), (0, 256, 512), (1, 0, 512))
+        for b, lo, hi in pieces:
             acc = psum.tile([P, hi - lo], F32, name="acc", bufs=3)
             for z in range(PASSES):
                 nc.tensor.matmul_mx(
@@ -96,7 +115,7 @@ def tile_picked_kvput_tanh_e_kernel(tc, xT, mem, w1_words, w1_scales, offs, slot
                 )
             nc.scalar.activation(y[b][:, lo:hi], acc[:], TANH)
 
-        for b, lo, hi in ((0, 0, 128), (1, 0, 256), (0, 128, 512), (1, 256, 512)):
+        for b, lo, hi in ((0, 0, 128), (0, 128, 512), (1, 0, 512)):
             nc.vector.tensor_copy(store[b][:].indirect(entries(slot_sb, lo, hi)), y[b][:, lo:hi])
             if hi == S:
                 nc.sync.dma_start(out[b * P : (b + 1) * P, :], store[b][:])

@@ -43,7 +43,12 @@ def tile_picked_kvput_tanh_e_kernel(tc, xT, mem, w1_words, w1_scales, offs, slot
         rounded = {j: keep.tile([P, T], BF16, name=f"rounded{j}") for j in (2, 3)}
         store = [keep.tile([P, U], F32, name=f"store{b}") for b in range(BLOCKS)]
 
-        nc.vector.memset(w_scales[:].rearrange("p z n -> p (z n)").bitcast(I32), 0)
+        nc.gpsimd.memset(w_scales[:].rearrange("p z n -> p (z n)").bitcast(I32), 0)
+        for q in range(4):
+            nc.gpsimd.dma_start(
+                w_scales[32 * q : 32 * q + 4].bitcast(I32),
+                w1_scales[:, 4 * q : 4 * q + 4, :].rearrange("z r n -> r z n").bitcast(I32),
+            )
         x_rows = xT.rearrange("(z p j) t -> z p j t", z=PASSES, j=PACK)
         nc.sync.dma_start(first_rows[:], x_rows[0, :, 0:2, :])
         nc.sync.dma_start(offs_sb[:], offs)
@@ -52,11 +57,6 @@ def tile_picked_kvput_tanh_e_kernel(tc, xT, mem, w1_words, w1_scales, offs, slot
             nc.sync.dma_start(rows[z, j], x_rows[z, :, j, :])
         for lo, hi in ((0, CUTS[2]), CUTS[2:4], CUTS[3:5]):
             nc.sync.dma_start(rows[1, 3][:, lo:hi], x_rows[1, :, 3, lo:hi])
-        for q in range(4):
-            nc.sync.dma_start(
-                w_scales[32 * q : 32 * q + 4].bitcast(I32),
-                w1_scales[:, 4 * q : 4 * q + 4, :].rearrange("z r n -> r z n").bitcast(I32),
-            )
         nc.sync.dma_start(w_codes[:].bitcast(I32), w1_words.rearrange("z p n r -> p z (n r)").bitcast(I32))
         for b in range(BLOCKS):
             nc.sync.dma_start(store[b][:], mem[b * P : (b + 1) * P, :])
@@ -102,7 +102,7 @@ def tile_picked_kvput_tanh_e_kernel(tc, xT, mem, w1_words, w1_scales, offs, slot
         y = [keep.tile([P, S], F32, name=f"y{b}") for b in range(BLOCKS)]
         pieces = ((0, 0, 128), (0, 128, 256), (0, 256, 512), (1, 0, 512))
         for b, lo, hi in pieces:
-            acc = psum.tile([P, hi - lo], F32, name="acc", bufs=3)
+            acc = psum.tile([P, hi - lo], F32, name=f"acc{hi}")
             for z in range(PASSES):
                 nc.tensor.matmul_mx(
                     out=acc[:],

@@ -22,7 +22,8 @@ BLOCKS = N // P
 HALVES = 2
 HALF = S // HALVES
 LANES = 16
-CUTS = (0, 768, 1280, 1792, 2048)
+VECTOR_CUT = 1024
+LAST_CUT = 1536
 
 
 def tile_picked_kvput_tanh_e_kernel(tc, xT, mem, w1_words, w1_scales, offs, slot, out):
@@ -35,12 +36,11 @@ def tile_picked_kvput_tanh_e_kernel(tc, xT, mem, w1_words, w1_scales, offs, slot
         slot_sb = keep.tile([P, S // LANES], U16, name="slot_sb")
         w_codes = keep.tile([P, PASSES, N], U32, name="w_codes", align_bytes=64)
         w_scales = keep.tile([P, PASSES, N], U8, name="w_scales", align_bytes=64)
-        first_rows = keep.tile([P, 2, T], F32, name="first_rows")
-        rows = {(0, j): first_rows[:, j, :] for j in range(2)}
-        later = [(0, 2), (0, 3), (1, 2), (1, 0), (1, 1), (1, 3)]
-        for z, j in later:
-            rows[z, j] = keep.tile([P, T], F32, name=f"rows{z}{j}")[:]
-        rounded = {j: keep.tile([P, T], BF16, name=f"rounded{j}") for j in (2, 3)}
+        pairs = [keep.tile([P, 2, T], F32, name=f"pair{u}") for u in range(2)]
+        rows = {(0, j): pairs[j // 2][:, j % 2, :] for j in range(PACK)}
+        for j in range(PACK):
+            rows[1, j] = keep.tile([P, T], F32, name=f"rows1{j}")[:]
+        rounded = keep.tile([P, T], BF16, name="rounded")
         store = [keep.tile([P, U], F32, name=f"store{b}") for b in range(BLOCKS)]
 
         nc.gpsimd.memset(w_scales[:].rearrange("p z n -> p (z n)").bitcast(I32), 0)
@@ -50,14 +50,15 @@ def tile_picked_kvput_tanh_e_kernel(tc, xT, mem, w1_words, w1_scales, offs, slot
                 w1_scales[:, 4 * q : 4 * q + 4, :].rearrange("z r n -> r z n").bitcast(I32),
             )
         x_rows = xT.rearrange("(z p j) t -> z p j t", z=PASSES, j=PACK)
-        nc.sync.dma_start(first_rows[:], x_rows[0, :, 0:2, :])
+        nc.sync.dma_start(pairs[0][:], x_rows[0, :, 0:2, :])
         nc.sync.dma_start(offs_sb[:], offs)
-        nc.sync.dma_start(slot_sb[:], slot)
-        for z, j in later[:-1]:
-            nc.sync.dma_start(rows[z, j], x_rows[z, :, j, :])
-        for lo, hi in ((0, CUTS[2]), CUTS[2:4], CUTS[3:5]):
+        nc.sync.dma_start(pairs[1][:], x_rows[0, :, 2:4, :])
+        for j in range(PACK - 1):
+            nc.sync.dma_start(rows[1, j], x_rows[1, :, j, :])
+        for lo, hi in ((0, LAST_CUT), (LAST_CUT, T)):
             nc.sync.dma_start(rows[1, 3][:, lo:hi], x_rows[1, :, 3, lo:hi])
         nc.sync.dma_start(w_codes[:].bitcast(I32), w1_words.rearrange("z p n r -> p z (n r)").bitcast(I32))
+        nc.sync.dma_start(slot_sb[:], slot)
         for b in range(BLOCKS):
             nc.sync.dma_start(store[b][:], mem[b * P : (b + 1) * P, :])
 
@@ -79,30 +80,24 @@ def tile_picked_kvput_tanh_e_kernel(tc, xT, mem, w1_words, w1_scales, offs, slot
             nc.vector.tensor_copy(picked0[:, :, j], rows[0, j].indirect(offs_sb[:]))
         quantize(0, picked0, 0, 0, S)
 
-        picked1 = [keep.tile([P, HALF, PACK], BF16, name=f"picked1{h}", align_bytes=64) for h in range(HALVES)]
-        half_list = [entries(offs_sb, h * HALF, (h + 1) * HALF) for h in range(HALVES)]
-
-        nc.scalar.activation(rounded[2][:], rows[1, 2], COPY)
-        nc.scalar.activation(picked1[1][:, :, 2], rounded[2][:].indirect(half_list[1]), COPY)
-        nc.vector.tensor_copy(picked1[0][:, :, 2], rows[1, 2].indirect(half_list[0]))
-        for j in range(2):
-            for h in range(HALVES):
-                nc.vector.tensor_copy(picked1[h][:, :, j], rows[1, j].indirect(half_list[h]))
-        for n in range(4):
-            lo, hi = CUTS[n : n + 2]
-            if n % 2 == 0:
-                nc.vector.tensor_copy(rounded[3][:, lo:hi], rows[1, 3][:, lo:hi])
-            else:
-                nc.scalar.activation(rounded[3][:, lo:hi], rows[1, 3][:, lo:hi], COPY)
-        nc.vector.tensor_copy(picked1[0][:, :, 3], rows[1, 3].indirect(half_list[0]))
-        nc.scalar.activation(picked1[1][:, :, 3], rounded[3][:].indirect(half_list[1]), COPY)
+        picked1 = keep.tile([P, S, PACK], BF16, name="picked1", align_bytes=64)
+        for j in range(PACK - 1):
+            nc.vector.tensor_copy(picked1[:, :, j], rows[1, j].indirect(offs_sb[:]))
+        last = rows[1, 3]
+        nc.vector.tensor_copy(rounded[:, 0:VECTOR_CUT], last[:, 0:VECTOR_CUT])
+        nc.scalar.activation(rounded[:, VECTOR_CUT:LAST_CUT], last[:, VECTOR_CUT:LAST_CUT], COPY)
+        nc.scalar.activation(rounded[:, LAST_CUT:T], last[:, LAST_CUT:T], COPY)
+        nc.vector.tensor_copy(picked1[:, 0:HALF, 3], last.indirect(entries(offs_sb, 0, HALF)))
+        nc.scalar.activation(picked1[:, HALF:S, 3], rounded[:].indirect(entries(offs_sb, HALF, S)), COPY)
         for lo, hi in ((0, 128), (128, 256), (256, 512)):
-            quantize(1, picked1[lo // HALF], lo // HALF * HALF, lo, hi)
+            quantize(1, picked1, 0, lo, hi)
 
-        y = [keep.tile([P, S], F32, name=f"y{b}") for b in range(BLOCKS)]
-        pieces = ((0, 0, 128), (0, 128, 256), (0, 256, 512), (1, 0, 512))
-        for b, lo, hi in pieces:
-            acc = psum.tile([P, hi - lo], F32, name=f"acc{hi}")
+        def results(b, lo, hi):
+            base = {(0, 0): LAST_CUT, (1, 0): LAST_CUT + 128}.get((b, lo), b * S + lo)
+            return last[:, base : base + hi - lo]
+
+        for b, lo, hi in ((0, 0, 128), (1, 0, 256), (0, 128, 256), (0, 256, 512), (1, 256, 512)):
+            acc = psum.tile([P, hi - lo], F32, name=f"acc{hi - lo}")
             for z in range(PASSES):
                 nc.tensor.matmul_mx(
                     out=acc[:],
@@ -113,9 +108,9 @@ def tile_picked_kvput_tanh_e_kernel(tc, xT, mem, w1_words, w1_scales, offs, slot
                     start=(z == 0),
                     stop=(z == PASSES - 1),
                 )
-            nc.scalar.activation(y[b][:, lo:hi], acc[:], TANH)
+            nc.scalar.activation(results(b, lo, hi), acc[:], TANH)
 
-        for b, lo, hi in ((0, 0, 128), (0, 128, 512), (1, 0, 512)):
-            nc.vector.tensor_copy(store[b][:].indirect(entries(slot_sb, lo, hi)), y[b][:, lo:hi])
+        for b, lo, hi in ((0, 0, 128), (1, 0, 256), (0, 128, 512), (1, 256, 512)):
+            nc.vector.tensor_copy(store[b][:].indirect(entries(slot_sb, lo, hi)), results(b, lo, hi))
             if hi == S:
                 nc.sync.dma_start(out[b * P : (b + 1) * P, :], store[b][:])

@@ -36,10 +36,11 @@ def tile_picked_kvput_tanh_e_kernel(tc, xT, mem, w1_words, w1_scales, offs, slot
         slot_sb = keep.tile([P, S // LANES], U16, name="slot_sb")
         w_codes = keep.tile([P, PASSES, N], U32, name="w_codes", align_bytes=64)
         w_scales = keep.tile([P, PASSES, N], U8, name="w_scales", align_bytes=64)
-        pairs = [keep.tile([P, 2, T], F32, name=f"pair{u}") for u in range(2)]
-        rows = {(0, j): pairs[j // 2][:, j % 2, :] for j in range(PACK)}
-        for j in range(PACK):
-            rows[1, j] = keep.tile([P, T], F32, name=f"rows1{j}")[:]
+        first_rows = keep.tile([P, 2, T], F32, name="first_rows")
+        rows = {(0, j): first_rows[:, j, :] for j in range(2)}
+        later = [(z, j) for z in range(PASSES) for j in range(PACK) if (z, j) not in rows]
+        for z, j in later:
+            rows[z, j] = keep.tile([P, T], F32, name=f"rows{z}{j}")[:]
         rounded = keep.tile([P, T], BF16, name="rounded")
         store = [keep.tile([P, U], F32, name=f"store{b}") for b in range(BLOCKS)]
 
@@ -50,11 +51,10 @@ def tile_picked_kvput_tanh_e_kernel(tc, xT, mem, w1_words, w1_scales, offs, slot
                 w1_scales[:, 4 * q : 4 * q + 4, :].rearrange("z r n -> r z n").bitcast(I32),
             )
         x_rows = xT.rearrange("(z p j) t -> z p j t", z=PASSES, j=PACK)
-        nc.sync.dma_start(pairs[0][:], x_rows[0, :, 0:2, :])
+        nc.sync.dma_start(first_rows[:], x_rows[0, :, 0:2, :])
         nc.sync.dma_start(offs_sb[:], offs)
-        nc.sync.dma_start(pairs[1][:], x_rows[0, :, 2:4, :])
-        for j in range(PACK - 1):
-            nc.sync.dma_start(rows[1, j], x_rows[1, :, j, :])
+        for z, j in later[:-1]:
+            nc.sync.dma_start(rows[z, j], x_rows[z, :, j, :])
         for lo, hi in ((0, LAST_CUT), (LAST_CUT, T)):
             nc.sync.dma_start(rows[1, 3][:, lo:hi], x_rows[1, :, 3, lo:hi])
         nc.sync.dma_start(w_codes[:].bitcast(I32), w1_words.rearrange("z p n r -> p z (n r)").bitcast(I32))

@@ -36,11 +36,8 @@ def tile_picked_kvput_tanh_e_kernel(tc, xT, mem, w1_words, w1_scales, offs, slot
         slot_sb = keep.tile([P, S // LANES], U16, name="slot_sb")
         w_codes = keep.tile([P, PASSES, N], U32, name="w_codes", align_bytes=64)
         w_scales = keep.tile([P, PASSES, N], U8, name="w_scales", align_bytes=64)
-        first_rows = keep.tile([P, 2, T], F32, name="first_rows")
-        rows = {(0, j): first_rows[:, j, :] for j in range(2)}
-        later = [(z, j) for z in range(PASSES) for j in range(PACK) if (z, j) not in rows]
-        for z, j in later:
-            rows[z, j] = keep.tile([P, T], F32, name=f"rows{z}{j}")[:]
+        planes = [(z, j) for z in range(PASSES) for j in range(PACK)]
+        rows = {(z, j): keep.tile([P, T], F32, name=f"rows{z}{j}")[:] for z, j in planes}
         rounded = keep.tile([P, T], BF16, name="rounded")
         store = [keep.tile([P, U], F32, name=f"store{b}") for b in range(BLOCKS)]
 
@@ -51,9 +48,9 @@ def tile_picked_kvput_tanh_e_kernel(tc, xT, mem, w1_words, w1_scales, offs, slot
                 w1_scales[:, 4 * q : 4 * q + 4, :].rearrange("z r n -> r z n").bitcast(I32),
             )
         x_rows = xT.rearrange("(z p j) t -> z p j t", z=PASSES, j=PACK)
-        nc.sync.dma_start(first_rows[:], x_rows[0, :, 0:2, :])
+        nc.sync.dma_start(rows[0, 0], x_rows[0, :, 0, :])
         nc.sync.dma_start(offs_sb[:], offs)
-        for z, j in later[:-1]:
+        for z, j in planes[1:-1]:
             nc.sync.dma_start(rows[z, j], x_rows[z, :, j, :])
         for lo, hi in ((0, LAST_CUT), (LAST_CUT, T)):
             nc.sync.dma_start(rows[1, 3][:, lo:hi], x_rows[1, :, 3, lo:hi])

@@ -22,8 +22,6 @@ BLOCKS = N // P
 HALVES = 2
 HALF = S // HALVES
 LANES = 16
-VECTOR_CUT = 1024
-LAST_CUT = 1536
 
 
 def tile_picked_kvput_tanh_e_kernel(tc, xT, mem, w1_words, w1_scales, offs, slot, out):
@@ -34,11 +32,10 @@ def tile_picked_kvput_tanh_e_kernel(tc, xT, mem, w1_words, w1_scales, offs, slot
 
         offs_sb = keep.tile([P, S // LANES], U16, name="offs_sb")
         slot_sb = keep.tile([P, S // LANES], U16, name="slot_sb")
-        w_codes = keep.tile([P, PASSES, N], U32, name="w_codes", align_bytes=64)
+        w_codes = [keep.tile([P, N], U32, name=f"w_codes{z}", align_bytes=64) for z in range(PASSES)]
         w_scales = keep.tile([P, PASSES, N], U8, name="w_scales", align_bytes=64)
         planes = [(z, j) for z in range(PASSES) for j in range(PACK)]
         rows = {(z, j): keep.tile([P, T], F32, name=f"rows{z}{j}")[:] for z, j in planes}
-        rounded = keep.tile([P, T], BF16, name="rounded")
         store = [keep.tile([P, U], F32, name=f"store{b}") for b in range(BLOCKS)]
 
         nc.gpsimd.memset(w_scales[:].rearrange("p z n -> p (z n)").bitcast(I32), 0)
@@ -50,11 +47,10 @@ def tile_picked_kvput_tanh_e_kernel(tc, xT, mem, w1_words, w1_scales, offs, slot
         x_rows = xT.rearrange("(z p j) t -> z p j t", z=PASSES, j=PACK)
         nc.sync.dma_start(rows[0, 0], x_rows[0, :, 0, :])
         nc.sync.dma_start(offs_sb[:], offs)
-        for z, j in planes[1:-1]:
+        for z, j in planes[1:]:
             nc.sync.dma_start(rows[z, j], x_rows[z, :, j, :])
-        for lo, hi in ((0, LAST_CUT), (LAST_CUT, T)):
-            nc.sync.dma_start(rows[1, 3][:, lo:hi], x_rows[1, :, 3, lo:hi])
-        nc.sync.dma_start(w_codes[:].bitcast(I32), w1_words.rearrange("z p n r -> p z (n r)").bitcast(I32))
+        for z in range(PASSES):
+            nc.sync.dma_start(w_codes[z][:].bitcast(I32), w1_words[z].rearrange("p n r -> p (n r)").bitcast(I32))
         nc.sync.dma_start(slot_sb[:], slot)
         for b in range(BLOCKS):
             nc.sync.dma_start(store[b][:], mem[b * P : (b + 1) * P, :])
@@ -65,49 +61,53 @@ def tile_picked_kvput_tanh_e_kernel(tc, xT, mem, w1_words, w1_scales, offs, slot
         x_codes = [keep.tile([P, S], U32, name=f"x_codes{z}", align_bytes=64) for z in range(PASSES)]
         x_scales = [keep.tile([P, S], U8, name=f"x_scales{z}", align_bytes=64) for z in range(PASSES)]
 
-        def quantize(z, picked, base, lo, hi):
+        def quantize(z, picked, lo, hi):
             nc.vector.quantize_mx(
                 out=x_codes[z][:, lo:hi].bitcast(FP8X4),
                 scales=x_scales[z][:, lo:hi],
-                in_=picked[:, lo - base : hi - base, :].rearrange("p s j -> p (s j)"),
+                in_=picked[:, lo:hi, :].rearrange("p s j -> p (s j)"),
             )
 
-        picked0 = keep.tile([P, S, PACK], BF16, name="picked0", align_bytes=64)
+        picked = [keep.tile([P, S, PACK], BF16, name=f"picked{z}", align_bytes=64) for z in range(PASSES)]
+        dense = [keep.tile([P, PACK, HALF], BF16, name=f"dense{z}") for z in range(PASSES)]
+
+        def gather(z, j):
+            nc.vector.tensor_copy(picked[z][:, 0:HALF, j], rows[z, j].indirect(entries(offs_sb, 0, HALF)))
+            nc.scalar.activation(dense[z][:, j, :], rows[z, j].indirect(entries(offs_sb, HALF, S)), COPY)
+
+        def woven(z, lo, hi):
+            return picked[z][:, HALF:S, lo:hi], dense[z][:, lo:hi, :].rearrange("p j s -> p s j")
+
         for j in range(PACK):
-            nc.vector.tensor_copy(picked0[:, :, j], rows[0, j].indirect(offs_sb[:]))
-        quantize(0, picked0, 0, 0, S)
-
-        picked1 = keep.tile([P, S, PACK], BF16, name="picked1", align_bytes=64)
+            gather(0, j)
+        nc.scalar.copy(*woven(0, 0, PACK))
+        quantize(0, picked[0], 0, S)
         for j in range(PACK - 1):
-            nc.vector.tensor_copy(picked1[:, :, j], rows[1, j].indirect(offs_sb[:]))
-        last = rows[1, 3]
-        nc.vector.tensor_copy(rounded[:, 0:VECTOR_CUT], last[:, 0:VECTOR_CUT])
-        nc.scalar.activation(rounded[:, VECTOR_CUT:LAST_CUT], last[:, VECTOR_CUT:LAST_CUT], COPY)
-        nc.scalar.activation(rounded[:, LAST_CUT:T], last[:, LAST_CUT:T], COPY)
-        nc.vector.tensor_copy(picked1[:, 0:HALF, 3], last.indirect(entries(offs_sb, 0, HALF)))
-        nc.scalar.activation(picked1[:, HALF:S, 3], rounded[:].indirect(entries(offs_sb, HALF, S)), COPY)
+            gather(1, j)
+        nc.scalar.copy(*woven(1, 0, PACK - 1))
+        gather(1, PACK - 1)
+        nc.vector.tensor_copy(*woven(1, PACK - 1, PACK))
         for lo, hi in ((0, 128), (128, 256), (256, 512)):
-            quantize(1, picked1, 0, lo, hi)
+            quantize(1, picked[1], lo, hi)
 
-        def results(b, lo, hi):
-            base = {(0, 0): LAST_CUT, (1, 0): LAST_CUT + 128}.get((b, lo), b * S + lo)
-            return last[:, base : base + hi - lo]
-
-        for b, lo, hi in ((0, 0, 128), (1, 0, 256), (0, 128, 256), (0, 256, 512), (1, 256, 512)):
-            acc = psum.tile([P, hi - lo], F32, name=f"acc{hi - lo}")
+        results = [keep.tile([P, S], F32, name=f"results{b}") for b in range(BLOCKS)]
+        for b, lo, hi in ((0, 0, 128), (0, 128, 256), (1, 0, 256), (0, 256, 512), (1, 256, 512)):
+            acc = psum.tile([P, hi - lo], F32, name=f"acc{b}_{lo}")
             for z in range(PASSES):
                 nc.tensor.matmul_mx(
                     out=acc[:],
-                    lhsT=w_codes[:, z, b * P : (b + 1) * P].bitcast(FP8X4),
+                    lhsT=w_codes[z][:, b * P : (b + 1) * P].bitcast(FP8X4),
                     lhsT_scale=w_scales[:, z, b * P : (b + 1) * P],
                     rhs=x_codes[z][:, lo:hi].bitcast(FP8X4),
                     rhs_scale=x_scales[z][:, lo:hi],
                     start=(z == 0),
                     stop=(z == PASSES - 1),
                 )
-            nc.scalar.activation(results(b, lo, hi), acc[:], TANH)
+            nc.scalar.activation(results[b][:, lo:hi], acc[:], TANH)
 
-        for b, lo, hi in ((0, 0, 128), (1, 0, 256), (0, 128, 512), (1, 256, 512)):
-            nc.vector.tensor_copy(store[b][:].indirect(entries(slot_sb, lo, hi)), results(b, lo, hi))
-            if hi == S:
-                nc.sync.dma_start(out[b * P : (b + 1) * P, :], store[b][:])
+        for lo, hi in ((0, 128), (128, 512)):
+            nc.vector.tensor_copy(store[0][:].indirect(entries(slot_sb, lo, hi)), results[0][:, lo:hi])
+        nc.sync.dma_start(out[0:P, :], store[0][:])
+        for lo, hi in ((0, 384), (384, 512)):
+            nc.scalar.activation(store[1][:].indirect(entries(slot_sb, lo, hi)), results[1][:, lo:hi], COPY)
+        nc.sync.dma_start(out[P : 2 * P, :], store[1][:])

@@ -22,6 +22,7 @@ BLOCKS = N // P
 HALVES = 2
 HALF = S // HALVES
 LANES = 16
+PIECE = 128
 
 
 def tile_picked_kvput_tanh_e_kernel(tc, xT, mem, w1_words, w1_scales, offs, slot, out):
@@ -69,7 +70,7 @@ def tile_picked_kvput_tanh_e_kernel(tc, xT, mem, w1_words, w1_scales, offs, slot
             )
 
         picked = [keep.tile([P, S, PACK], BF16, name=f"picked{z}", align_bytes=64) for z in range(PASSES)]
-        dense = [keep.tile([P, PACK, HALF], BF16, name=f"dense{z}") for z in range(PASSES)]
+        dense = [keep.tile([P, PACK - z, HALF], BF16, name=f"dense{z}") for z in range(PASSES)]
 
         def gather(z, j):
             nc.vector.tensor_copy(picked[z][:, 0:HALF, j], rows[z, j].indirect(entries(offs_sb, 0, HALF)))
@@ -85,17 +86,38 @@ def tile_picked_kvput_tanh_e_kernel(tc, xT, mem, w1_words, w1_scales, offs, slot
         for j in range(PACK - 1):
             gather(1, j)
         nc.scalar.copy(*woven(1, 0, PACK - 1))
-        gather(1, PACK - 1)
-        nc.vector.tensor_copy(*woven(1, PACK - 1, PACK))
-        for lo, hi in ((0, 128), (128, 256), (256, 512)):
-            quantize(1, picked[1], lo, hi)
+        last = rows[1, PACK - 1]
+        tail = keep.tile([P, S], BF16, name="tail")
+
+        def piece(q):
+            return slice(q * PIECE, (q + 1) * PIECE)
+
+        def fetched(q):
+            return tail[:, piece(q)], last.indirect(entries(offs_sb, q * PIECE, (q + 1) * PIECE))
+
+        def placed(q):
+            return picked[1][:, piece(q), PACK - 1], tail[:, piece(q)]
+
+        nc.vector.tensor_copy(*fetched(0))
+        nc.vector.tensor_copy(*fetched(1))
+        nc.scalar.activation(*fetched(2), COPY)
+        nc.scalar.activation(*fetched(3), COPY)
+        nc.scalar.copy(*placed(2))
+        nc.vector.tensor_copy(*placed(0))
+        nc.vector.tensor_copy(*placed(1))
+        quantize(1, picked[1], 0, PIECE)
+        quantize(1, picked[1], PIECE, 2 * PIECE)
+        nc.vector.tensor_copy(*placed(3))
+        quantize(1, picked[1], 2 * PIECE, 3 * PIECE)
+        quantize(1, picked[1], 3 * PIECE, S)
 
         results = [keep.tile([P, S], F32, name=f"results{b}") for b in range(BLOCKS)]
-        for b, lo, hi in ((0, 0, 128), (0, 128, 256), (1, 0, 256), (0, 256, 512), (1, 256, 512)):
-            acc = psum.tile([P, hi - lo], F32, name=f"acc{b}_{lo}")
-            for z in range(PASSES):
+        groups = ((0, 0, 128), (0, 128, 256), (1, 0, 256), (0, 256, 384), (1, 256, 512), (0, 384, 512))
+        acc = {(b, lo): psum.tile([P, hi - lo], F32, name=f"acc{b}_{lo}") for b, lo, hi in groups}
+        for z in range(PASSES):
+            for b, lo, hi in groups:
                 nc.tensor.matmul_mx(
-                    out=acc[:],
+                    out=acc[b, lo][:],
                     lhsT=w_codes[z][:, b * P : (b + 1) * P].bitcast(FP8X4),
                     lhsT_scale=w_scales[:, z, b * P : (b + 1) * P],
                     rhs=x_codes[z][:, lo:hi].bitcast(FP8X4),
@@ -103,7 +125,8 @@ def tile_picked_kvput_tanh_e_kernel(tc, xT, mem, w1_words, w1_scales, offs, slot
                     start=(z == 0),
                     stop=(z == PASSES - 1),
                 )
-            nc.scalar.activation(results[b][:, lo:hi], acc[:], TANH)
+        for b, lo, hi in groups:
+            nc.scalar.activation(results[b][:, lo:hi], acc[b, lo][:], TANH)
 
         for lo, hi in ((0, 128), (128, 512)):
             nc.vector.tensor_copy(store[0][:].indirect(entries(slot_sb, lo, hi)), results[0][:, lo:hi])

@@ -35,8 +35,9 @@ def tile_picked_kvput_tanh_e_kernel(tc, xT, mem, w1_words, w1_scales, offs, slot
         slot_sb = keep.tile([P, S // LANES], U16, name="slot_sb")
         w_codes = [keep.tile([P, N], U32, name=f"w_codes{z}", align_bytes=64) for z in range(PASSES)]
         w_scales = keep.tile([P, PASSES, N], U8, name="w_scales", align_bytes=64)
-        planes = [(z, j) for z in range(PASSES) for j in range(PACK)]
-        rows = {(z, j): keep.tile([P, T], F32, name=f"rows{z}{j}")[:] for z, j in planes}
+        loads = ((0, 0, 2), (0, 2, 4), (1, 0, 2), (1, 2, 3), (1, 3, 4))
+        slabs = [keep.tile([P, hi - lo, T], F32, name=f"rows{z}{lo}") for z, lo, hi in loads]
+        rows = {(z, j): slab[:, j - lo, :] for slab, (z, lo, hi) in zip(slabs, loads) for j in range(lo, hi)}
         store = [keep.tile([P, U], F32, name=f"store{b}") for b in range(BLOCKS)]
 
         nc.gpsimd.memset(w_scales[:].rearrange("p z n -> p (z n)").bitcast(I32), 0)
@@ -46,10 +47,10 @@ def tile_picked_kvput_tanh_e_kernel(tc, xT, mem, w1_words, w1_scales, offs, slot
                 w1_scales[:, 4 * q : 4 * q + 4, :].rearrange("z r n -> r z n").bitcast(I32),
             )
         x_rows = xT.rearrange("(z p j) t -> z p j t", z=PASSES, j=PACK)
-        nc.sync.dma_start(rows[0, 0], x_rows[0, :, 0, :])
-        nc.sync.dma_start(offs_sb[:], offs)
-        for z, j in planes[1:]:
-            nc.sync.dma_start(rows[z, j], x_rows[z, :, j, :])
+        for n, (z, lo, hi) in enumerate(loads):
+            nc.sync.dma_start(slabs[n][:], x_rows[z, :, lo:hi, :])
+            if n == 0:
+                nc.sync.dma_start(offs_sb[:], offs)
         for z in range(PASSES):
             nc.sync.dma_start(w_codes[z][:].bitcast(I32), w1_words[z].rearrange("p n r -> p (n r)").bitcast(I32))
         nc.sync.dma_start(slot_sb[:], slot)
@@ -70,7 +71,7 @@ def tile_picked_kvput_tanh_e_kernel(tc, xT, mem, w1_words, w1_scales, offs, slot
             )
 
         picked = [keep.tile([P, S, PACK], BF16, name=f"picked{z}", align_bytes=64) for z in range(PASSES)]
-        dense = [keep.tile([P, PACK - z, HALF], BF16, name=f"dense{z}") for z in range(PASSES)]
+        dense = [keep.tile([P, PACK - z, HALF], F32, name=f"dense{z}") for z in range(PASSES)]
 
         def gather(z, j):
             nc.vector.tensor_copy(picked[z][:, 0:HALF, j], rows[z, j].indirect(entries(offs_sb, 0, HALF)))

@@ -40,9 +40,9 @@ def tile_picked_kvput_tanh_e_kernel(tc, xT, mem, w1_words, w1_scales, offs, slot
         rows = {(z, j): slab[:, j - lo, :] for slab, (z, lo, hi) in zip(slabs, loads) for j in range(lo, hi)}
         store = [keep.tile([P, U], F32, name=f"store{b}") for b in range(BLOCKS)]
 
-        nc.gpsimd.memset(w_scales[:].rearrange("p z n -> p (z n)").bitcast(I32), 0)
+        nc.vector.memset(w_scales[:].rearrange("p z n -> p (z n)").bitcast(I32), 0)
         for q in range(4):
-            nc.gpsimd.dma_start(
+            nc.scalar.dma_start(
                 w_scales[32 * q : 32 * q + 4].bitcast(I32),
                 w1_scales[:, 4 * q : 4 * q + 4, :].rearrange("z r n -> r z n").bitcast(I32),
             )

@@ -99,39 +99,42 @@ def tile_picked_kvput_tanh_e_kernel(tc, xT, mem, w1_words, w1_scales, offs, slot
         def placed(q):
             return picked[1][:, piece(q), PACK - 1], tail[:, piece(q)]
 
-        nc.vector.tensor_copy(*fetched(0))
+        nc.vector.tensor_copy(tail[:, 0:64], last.indirect(entries(offs_sb, 0, 64)))
+        nc.scalar.activation(tail[:, 64:PIECE], last.indirect(entries(offs_sb, 64, PIECE)), COPY)
         nc.vector.tensor_copy(*fetched(1))
         nc.scalar.activation(*fetched(2), COPY)
         nc.scalar.activation(*fetched(3), COPY)
         nc.scalar.copy(*placed(2))
+        nc.scalar.copy(*placed(3))
         nc.vector.tensor_copy(*placed(0))
         nc.vector.tensor_copy(*placed(1))
         quantize(1, picked[1], 0, PIECE)
         quantize(1, picked[1], PIECE, 2 * PIECE)
-        nc.vector.tensor_copy(*placed(3))
         quantize(1, picked[1], 2 * PIECE, 3 * PIECE)
         quantize(1, picked[1], 3 * PIECE, S)
 
         results = [keep.tile([P, S], F32, name=f"results{b}") for b in range(BLOCKS)]
-        groups = ((0, 0, 128), (0, 128, 256), (1, 0, 256), (0, 256, 384), (1, 256, 512), (0, 384, 512))
-        acc = {(b, lo): psum.tile([P, hi - lo], F32, name=f"acc{b}_{lo}") for b, lo, hi in groups}
-        for z in range(PASSES):
-            for b, lo, hi in groups:
-                nc.tensor.matmul_mx(
-                    out=acc[b, lo][:],
-                    lhsT=w_codes[z][:, b * P : (b + 1) * P].bitcast(FP8X4),
-                    lhsT_scale=w_scales[:, z, b * P : (b + 1) * P],
-                    rhs=x_codes[z][:, lo:hi].bitcast(FP8X4),
-                    rhs_scale=x_scales[z][:, lo:hi],
-                    start=(z == 0),
-                    stop=(z == PASSES - 1),
-                )
-        for b, lo, hi in groups:
-            nc.scalar.activation(results[b][:, lo:hi], acc[b, lo][:], TANH)
+        groups = ((0, 0, 128), (0, 128, 256), (1, 0, 256), (0, 256, 384), (0, 384, 512), (1, 256, 512))
+        acc = [psum.tile([P, hi - lo], F32, name=f"acc{b}_{lo}") for b, lo, hi in groups]
+        opened = set()
+        for g, z in ((0, 0), (1, 0), (3, 0), (4, 0), (5, 0), (0, 1), (2, 1), (1, 1), (2, 0), (3, 1), (4, 1), (5, 1)):
+            b, lo, hi = groups[g]
+            nc.tensor.matmul_mx(
+                out=acc[g][:],
+                lhsT=w_codes[z][:, b * P : (b + 1) * P].bitcast(FP8X4),
+                lhsT_scale=w_scales[:, z, b * P : (b + 1) * P],
+                rhs=x_codes[z][:, lo:hi].bitcast(FP8X4),
+                rhs_scale=x_scales[z][:, lo:hi],
+                start=(g not in opened),
+                stop=(g in opened),
+            )
+            if g in opened:
+                nc.scalar.activation(results[b][:, lo:hi], acc[g][:], TANH)
+            opened.add(g)
 
         for lo, hi in ((0, 128), (128, 512)):
             nc.vector.tensor_copy(store[0][:].indirect(entries(slot_sb, lo, hi)), results[0][:, lo:hi])
         nc.sync.dma_start(out[0:P, :], store[0][:])
-        for lo, hi in ((0, 384), (384, 512)):
+        for lo, hi in ((0, 256), (256, 512)):
             nc.scalar.activation(store[1][:].indirect(entries(slot_sb, lo, hi)), results[1][:, lo:hi], COPY)
         nc.sync.dma_start(out[P : 2 * P, :], store[1][:])

@@ -35,7 +35,7 @@ def tile_picked_kvput_tanh_e_kernel(tc, xT, mem, w1_words, w1_scales, offs, slot
         slot_sb = keep.tile([P, S // LANES], U16, name="slot_sb")
         w_codes = [keep.tile([P, N], U32, name=f"w_codes{z}", align_bytes=64) for z in range(PASSES)]
         w_scales = keep.tile([P, PASSES, N], U8, name="w_scales", align_bytes=64)
-        loads = ((0, 0, 2), (0, 2, 4), (1, 0, 2), (1, 2, 3), (1, 3, 4))
+        loads = ((0, 0, 4), (1, 0, 2), (1, 2, 3), (1, 3, 4))
         slabs = [keep.tile([P, hi - lo, T], F32, name=f"rows{z}{lo}") for z, lo, hi in loads]
         rows = {(z, j): slab[:, j - lo, :] for slab, (z, lo, hi) in zip(slabs, loads) for j in range(lo, hi)}
         store = [keep.tile([P, U], F32, name=f"store{b}") for b in range(BLOCKS)]

@@ -19,10 +19,10 @@ P = 128
 PACK = 4
 PASSES = K // (P * PACK)
 BLOCKS = N // P
-HALVES = 2
-HALF = S // HALVES
 LANES = 16
+HALF = S // 2
 PIECE = 128
+LOADS = ((0, 0, 4), (1, 0, 2), (1, 2, 3), (1, 3, 4))
 
 
 def tile_picked_kvput_tanh_e_kernel(tc, xT, mem, w1_words, w1_scales, offs, slot, out):
@@ -35,10 +35,9 @@ def tile_picked_kvput_tanh_e_kernel(tc, xT, mem, w1_words, w1_scales, offs, slot
         slot_sb = keep.tile([P, S // LANES], U16, name="slot_sb")
         w_codes = [keep.tile([P, N], U32, name=f"w_codes{z}", align_bytes=64) for z in range(PASSES)]
         w_scales = keep.tile([P, PASSES, N], U8, name="w_scales", align_bytes=64)
-        loads = ((0, 0, 4), (1, 0, 2), (1, 2, 3), (1, 3, 4))
-        slabs = [keep.tile([P, hi - lo, T], F32, name=f"rows{z}{lo}") for z, lo, hi in loads]
-        rows = {(z, j): slab[:, j - lo, :] for slab, (z, lo, hi) in zip(slabs, loads) for j in range(lo, hi)}
-        store = [keep.tile([P, U], F32, name=f"store{b}") for b in range(BLOCKS)]
+        slabs = [keep.tile([P, hi - lo, T], F32, name=f"slab{z}{lo}") for z, lo, hi in LOADS]
+        plane = {(z, j): slab[:, j - lo, :] for slab, (z, lo, hi) in zip(slabs, LOADS) for j in range(lo, hi)}
+        window = [keep.tile([P, U], F32, name=f"window{b}") for b in range(BLOCKS)]
 
         nc.vector.memset(w_scales[:].rearrange("p z n -> p (z n)").bitcast(I32), 0)
         for q in range(4):
@@ -47,7 +46,7 @@ def tile_picked_kvput_tanh_e_kernel(tc, xT, mem, w1_words, w1_scales, offs, slot
                 w1_scales[:, 4 * q : 4 * q + 4, :].rearrange("z r n -> r z n").bitcast(I32),
             )
         x_rows = xT.rearrange("(z p j) t -> z p j t", z=PASSES, j=PACK)
-        for n, (z, lo, hi) in enumerate(loads):
+        for n, (z, lo, hi) in enumerate(LOADS):
             nc.sync.dma_start(slabs[n][:], x_rows[z, :, lo:hi, :])
             if n == 0:
                 nc.sync.dma_start(offs_sb[:], offs)
@@ -55,63 +54,55 @@ def tile_picked_kvput_tanh_e_kernel(tc, xT, mem, w1_words, w1_scales, offs, slot
             nc.sync.dma_start(w_codes[z][:].bitcast(I32), w1_words[z].rearrange("p n r -> p (n r)").bitcast(I32))
         nc.sync.dma_start(slot_sb[:], slot)
         for b in range(BLOCKS):
-            nc.sync.dma_start(store[b][:], mem[b * P : (b + 1) * P, :])
+            nc.sync.dma_start(window[b][:], mem[b * P : (b + 1) * P, :])
 
         def entries(list_tile, lo, hi):
             return list_tile[:, lo // LANES : hi // LANES]
 
+        picked = [keep.tile([P, S, PACK], BF16, name=f"picked{z}", align_bytes=64) for z in range(PASSES)]
         x_codes = [keep.tile([P, S], U32, name=f"x_codes{z}", align_bytes=64) for z in range(PASSES)]
         x_scales = [keep.tile([P, S], U8, name=f"x_scales{z}", align_bytes=64) for z in range(PASSES)]
+        dense = [keep.tile([P, PACK // (z + 1), HALF], F32, name=f"dense{z}") for z in range(PASSES)]
+        last_pair = keep.tile([P, 2, S], BF16, name="last_pair")
 
-        def quantize(z, picked, lo, hi):
+        def quantize(z, lo, hi):
             nc.vector.quantize_mx(
                 out=x_codes[z][:, lo:hi].bitcast(FP8X4),
                 scales=x_scales[z][:, lo:hi],
-                in_=picked[:, lo:hi, :].rearrange("p s j -> p (s j)"),
+                in_=picked[z][:, lo:hi, :].rearrange("p s j -> p (s j)"),
             )
 
-        picked = [keep.tile([P, S, PACK], BF16, name=f"picked{z}", align_bytes=64) for z in range(PASSES)]
-        dense = [keep.tile([P, PACK - z, HALF], F32, name=f"dense{z}") for z in range(PASSES)]
-
         def gather(z, j):
-            nc.vector.tensor_copy(picked[z][:, 0:HALF, j], rows[z, j].indirect(entries(offs_sb, 0, HALF)))
-            nc.scalar.activation(dense[z][:, j, :], rows[z, j].indirect(entries(offs_sb, HALF, S)), COPY)
+            nc.vector.tensor_copy(picked[z][:, 0:HALF, j], plane[z, j].indirect(entries(offs_sb, 0, HALF)))
+            nc.scalar.activation(dense[z][:, j, :], plane[z, j].indirect(entries(offs_sb, HALF, S)), COPY)
 
-        def woven(z, lo, hi):
-            return picked[z][:, HALF:S, lo:hi], dense[z][:, lo:hi, :].rearrange("p j s -> p s j")
+        def fetched(j, lo, hi):
+            return last_pair[:, j - 2, lo:hi], plane[1, j].indirect(entries(offs_sb, lo, hi))
+
+        def placed(lo, hi):
+            return picked[1][:, lo:hi, 2:PACK], last_pair[:, :, lo:hi].rearrange("p j s -> p s j")
 
         for j in range(PACK):
             gather(0, j)
-        nc.scalar.copy(*woven(0, 0, PACK))
-        quantize(0, picked[0], 0, S)
-        for j in range(PACK - 1):
+        nc.vector.tensor_copy(picked[0][:, HALF:S, :], dense[0][:].rearrange("p j s -> p s j"))
+        quantize(0, 0, S)
+        for j in range(2):
             gather(1, j)
-        nc.scalar.copy(*woven(1, 0, PACK - 1))
-        last = rows[1, PACK - 1]
-        tail = keep.tile([P, S], BF16, name="tail")
+        nc.scalar.copy(picked[1][:, HALF:S, 0:2], dense[1][:].rearrange("p j s -> p s j"))
+        nc.vector.tensor_copy(*fetched(2, 0, HALF))
+        nc.scalar.activation(*fetched(2, HALF, S), COPY)
 
-        def piece(q):
-            return slice(q * PIECE, (q + 1) * PIECE)
-
-        def fetched(q):
-            return tail[:, piece(q)], last.indirect(entries(offs_sb, q * PIECE, (q + 1) * PIECE))
-
-        def placed(q):
-            return picked[1][:, piece(q), PACK - 1], tail[:, piece(q)]
-
-        nc.vector.tensor_copy(tail[:, 0:64], last.indirect(entries(offs_sb, 0, 64)))
-        nc.scalar.activation(tail[:, 64:PIECE], last.indirect(entries(offs_sb, 64, PIECE)), COPY)
-        nc.vector.tensor_copy(*fetched(1))
-        nc.scalar.activation(*fetched(2), COPY)
-        nc.scalar.activation(*fetched(3), COPY)
-        nc.scalar.copy(*placed(2))
-        nc.scalar.copy(*placed(3))
-        nc.vector.tensor_copy(*placed(0))
-        nc.vector.tensor_copy(*placed(1))
-        quantize(1, picked[1], 0, PIECE)
-        quantize(1, picked[1], PIECE, 2 * PIECE)
-        quantize(1, picked[1], 2 * PIECE, 3 * PIECE)
-        quantize(1, picked[1], 3 * PIECE, S)
+        nc.vector.tensor_copy(*fetched(3, 0, PIECE // 2))
+        nc.scalar.activation(*fetched(3, PIECE // 2, PIECE), COPY)
+        nc.vector.tensor_copy(*fetched(3, PIECE, HALF))
+        nc.scalar.activation(*fetched(3, HALF, HALF + PIECE), COPY)
+        nc.scalar.activation(*fetched(3, HALF + PIECE, S), COPY)
+        nc.scalar.copy(*placed(HALF, HALF + PIECE))
+        nc.scalar.copy(*placed(HALF + PIECE, S))
+        nc.vector.tensor_copy(*placed(0, PIECE))
+        nc.vector.tensor_copy(*placed(PIECE, HALF))
+        for lo in range(0, S, PIECE):
+            quantize(1, lo, lo + PIECE)
 
         results = [keep.tile([P, S], F32, name=f"results{b}") for b in range(BLOCKS)]
         groups = ((0, 0, 128), (0, 128, 256), (1, 0, 256), (0, 256, 384), (0, 384, 512), (1, 256, 512))
@@ -132,9 +123,9 @@ def tile_picked_kvput_tanh_e_kernel(tc, xT, mem, w1_words, w1_scales, offs, slot
                 nc.scalar.activation(results[b][:, lo:hi], acc[g][:], TANH)
             opened.add(g)
 
-        for lo, hi in ((0, 128), (128, 512)):
-            nc.vector.tensor_copy(store[0][:].indirect(entries(slot_sb, lo, hi)), results[0][:, lo:hi])
-        nc.sync.dma_start(out[0:P, :], store[0][:])
-        for lo, hi in ((0, 256), (256, 512)):
-            nc.scalar.activation(store[1][:].indirect(entries(slot_sb, lo, hi)), results[1][:, lo:hi], COPY)
-        nc.sync.dma_start(out[P : 2 * P, :], store[1][:])
+        for lo, hi in ((0, PIECE), (PIECE, S)):
+            nc.vector.tensor_copy(window[0][:].indirect(entries(slot_sb, lo, hi)), results[0][:, lo:hi])
+        nc.sync.dma_start(out[0:P, :], window[0][:])
+        for lo, hi in ((0, HALF), (HALF, S)):
+            nc.scalar.activation(window[1][:].indirect(entries(slot_sb, lo, hi)), results[1][:, lo:hi], COPY)
+        nc.sync.dma_start(out[P : 2 * P, :], window[1][:])

@@ -84,13 +84,14 @@ def tile_picked_kvput_tanh_e_kernel(tc, xT, mem, w1_words, w1_scales, offs, slot
 
         for j in range(PACK):
             gather(0, j)
+        quantize(0, 0, HALF)
         nc.vector.tensor_copy(picked[0][:, HALF:S, :], dense[0][:].rearrange("p j s -> p s j"))
-        quantize(0, 0, S)
+        quantize(0, HALF, S)
         for j in range(2):
             gather(1, j)
         nc.scalar.copy(picked[1][:, HALF:S, 0:2], dense[1][:].rearrange("p j s -> p s j"))
-        nc.vector.tensor_copy(*fetched(2, 0, HALF))
-        nc.scalar.activation(*fetched(2, HALF, S), COPY)
+        nc.vector.tensor_copy(*fetched(2, 0, PIECE))
+        nc.scalar.activation(*fetched(2, PIECE, S), COPY)
 
         nc.vector.tensor_copy(*fetched(3, 0, PIECE // 2))
         nc.scalar.activation(*fetched(3, PIECE // 2, PIECE), COPY)

@@ -109,7 +109,7 @@ def tile_picked_kvput_tanh_e_kernel(tc, xT, mem, w1_words, w1_scales, offs, slot
         groups = ((0, 0, 128), (0, 128, 256), (1, 0, 256), (0, 256, 384), (0, 384, 512), (1, 256, 512))
         acc = [psum.tile([P, hi - lo], F32, name=f"acc{b}_{lo}") for b, lo, hi in groups]
         opened = set()
-        for g, z in ((0, 0), (1, 0), (3, 0), (4, 0), (5, 0), (0, 1), (2, 1), (1, 1), (2, 0), (3, 1), (4, 1), (5, 1)):
+        for g, z in ((0, 0), (2, 0), (3, 0), (4, 0), (5, 0), (0, 1), (1, 1), (2, 1), (1, 0), (3, 1), (4, 1), (5, 1)):
             b, lo, hi = groups[g]
             nc.tensor.matmul_mx(
                 out=acc[g][:],

@@ -39,12 +39,15 @@ def tile_picked_kvput_tanh_e_kernel(tc, xT, mem, w1_words, w1_scales, offs, slot
         plane = {(z, j): slab[:, j - lo, :] for slab, (z, lo, hi) in zip(slabs, LOADS) for j in range(lo, hi)}
         window = [keep.tile([P, U], F32, name=f"window{b}") for b in range(BLOCKS)]
 
-        nc.vector.memset(w_scales[:].rearrange("p z n -> p (z n)").bitcast(I32), 0)
+        staged = keep.tile([P, PASSES, N], U8, name="staged")
+        nc.gpsimd.memset(w_scales[:].rearrange("p z n -> p (z n)").bitcast(I32), 0)
         for q in range(4):
+            live = slice(32 * q, 32 * q + 4)
             nc.scalar.dma_start(
-                w_scales[32 * q : 32 * q + 4].bitcast(I32),
+                staged[live].bitcast(I32),
                 w1_scales[:, 4 * q : 4 * q + 4, :].rearrange("z r n -> r z n").bitcast(I32),
             )
+            nc.gpsimd.tensor_copy(w_scales[live].bitcast(I32), staged[live].bitcast(I32))
         x_rows = xT.rearrange("(z p j) t -> z p j t", z=PASSES, j=PACK)
         for n, (z, lo, hi) in enumerate(LOADS):
             nc.sync.dma_start(slabs[n][:], x_rows[z, :, lo:hi, :])

@@ -39,15 +39,14 @@ def tile_picked_kvput_tanh_e_kernel(tc, xT, mem, w1_words, w1_scales, offs, slot
         plane = {(z, j): slab[:, j - lo, :] for slab, (z, lo, hi) in zip(slabs, LOADS) for j in range(lo, hi)}
         window = [keep.tile([P, U], F32, name=f"window{b}") for b in range(BLOCKS)]
 
-        staged = keep.tile([P, PASSES, N], U8, name="staged")
-        nc.gpsimd.memset(w_scales[:].rearrange("p z n -> p (z n)").bitcast(I32), 0)
+        staged = keep.tile([4, PASSES, 4, N], U8, name="staged")
+        nc.scalar.dma_start(
+            staged[:].rearrange("r z q n -> r (z q) n").bitcast(I32),
+            w1_scales.rearrange("z (q r) n -> r (z q) n", r=4).bitcast(I32),
+        )
+        nc.vector.memset(w_scales[:].rearrange("p z n -> p (z n)").bitcast(I32), 0)
         for q in range(4):
-            live = slice(32 * q, 32 * q + 4)
-            nc.scalar.dma_start(
-                staged[live].bitcast(I32),
-                w1_scales[:, 4 * q : 4 * q + 4, :].rearrange("z r n -> r z n").bitcast(I32),
-            )
-            nc.gpsimd.tensor_copy(w_scales[live].bitcast(I32), staged[live].bitcast(I32))
+            nc.vector.tensor_copy(w_scales[32 * q : 32 * q + 4].bitcast(I32), staged[:, :, q, :].bitcast(I32))
         x_rows = xT.rearrange("(z p j) t -> z p j t", z=PASSES, j=PACK)
         for n, (z, lo, hi) in enumerate(LOADS):
             nc.sync.dma_start(slabs[n][:], x_rows[z, :, lo:hi, :])

@@ -38,15 +38,18 @@ def tile_picked_kvput_tanh_e_kernel(tc, xT, mem, w1_words, w1_scales, offs, slot
         slabs = [keep.tile([P, hi - lo, T], F32, name=f"slab{z}{lo}") for z, lo, hi in LOADS]
         plane = {(z, j): slab[:, j - lo, :] for slab, (z, lo, hi) in zip(slabs, LOADS) for j in range(lo, hi)}
         window = [keep.tile([P, U], F32, name=f"window{b}") for b in range(BLOCKS)]
+        ones = keep.tile([P, 1], F32, name="ones")
 
-        staged = keep.tile([4, PASSES, 4, N], U8, name="staged")
-        nc.scalar.dma_start(
-            staged[:].rearrange("r z q n -> r (z q) n").bitcast(I32),
-            w1_scales.rearrange("z (q r) n -> r (z q) n", r=4).bitcast(I32),
-        )
-        nc.vector.memset(w_scales[:].rearrange("p z n -> p (z n)").bitcast(I32), 0)
+        staged = keep.tile([P, PASSES, N], U8, name="staged")
+        nc.gpsimd.memset(w_scales[:].rearrange("p z n -> p (z n)").bitcast(I32), 0)
         for q in range(4):
-            nc.vector.tensor_copy(w_scales[32 * q : 32 * q + 4].bitcast(I32), staged[:, :, q, :].bitcast(I32))
+            live = slice(32 * q, 32 * q + 4)
+            nc.scalar.dma_start(
+                staged[live].bitcast(I32),
+                w1_scales[:, 4 * q : 4 * q + 4, :].rearrange("z r n -> r z n").bitcast(I32),
+            )
+            nc.gpsimd.tensor_copy(w_scales[live].bitcast(I32), staged[live].bitcast(I32))
+        nc.vector.memset(ones[:], 1.0)
         x_rows = xT.rearrange("(z p j) t -> z p j t", z=PASSES, j=PACK)
         for n, (z, lo, hi) in enumerate(LOADS):
             nc.sync.dma_start(slabs[n][:], x_rows[z, :, lo:hi, :])
@@ -61,11 +64,14 @@ def tile_picked_kvput_tanh_e_kernel(tc, xT, mem, w1_words, w1_scales, offs, slot
         def entries(list_tile, lo, hi):
             return list_tile[:, lo // LANES : hi // LANES]
 
+        def looked_up(z, j, lo, hi):
+            return plane[z, j].indirect(entries(offs_sb, lo, hi))
+
         picked = [keep.tile([P, S, PACK], BF16, name=f"picked{z}", align_bytes=64) for z in range(PASSES)]
         x_codes = [keep.tile([P, S], U32, name=f"x_codes{z}", align_bytes=64) for z in range(PASSES)]
         x_scales = [keep.tile([P, S], U8, name=f"x_scales{z}", align_bytes=64) for z in range(PASSES)]
         dense = [keep.tile([P, PACK // (z + 1), HALF], F32, name=f"dense{z}") for z in range(PASSES)]
-        last_pair = keep.tile([P, 2, S], BF16, name="last_pair")
+        last_pair = keep.tile([P, 2, PIECE], BF16, name="last_pair")
 
         def quantize(z, lo, hi):
             nc.vector.quantize_mx(
@@ -75,14 +81,8 @@ def tile_picked_kvput_tanh_e_kernel(tc, xT, mem, w1_words, w1_scales, offs, slot
             )
 
         def gather(z, j):
-            nc.vector.tensor_copy(picked[z][:, 0:HALF, j], plane[z, j].indirect(entries(offs_sb, 0, HALF)))
-            nc.scalar.activation(dense[z][:, j, :], plane[z, j].indirect(entries(offs_sb, HALF, S)), COPY)
-
-        def fetched(j, lo, hi):
-            return last_pair[:, j - 2, lo:hi], plane[1, j].indirect(entries(offs_sb, lo, hi))
-
-        def placed(lo, hi):
-            return picked[1][:, lo:hi, 2:PACK], last_pair[:, :, lo:hi].rearrange("p j s -> p s j")
+            nc.vector.tensor_copy(picked[z][:, 0:HALF, j], looked_up(z, j, 0, HALF))
+            nc.scalar.activation(dense[z][:, j, :], looked_up(z, j, HALF, S), COPY)
 
         for j in range(PACK):
             gather(0, j)
@@ -92,43 +92,49 @@ def tile_picked_kvput_tanh_e_kernel(tc, xT, mem, w1_words, w1_scales, offs, slot
         for j in range(2):
             gather(1, j)
         nc.scalar.copy(picked[1][:, HALF:S, 0:2], dense[1][:].rearrange("p j s -> p s j"))
-        nc.vector.tensor_copy(*fetched(2, 0, PIECE))
-        nc.scalar.activation(*fetched(2, PIECE, S), COPY)
 
-        nc.vector.tensor_copy(*fetched(3, 0, PIECE // 2))
-        nc.scalar.activation(*fetched(3, PIECE // 2, PIECE), COPY)
-        nc.vector.tensor_copy(*fetched(3, PIECE, HALF))
-        nc.scalar.activation(*fetched(3, HALF, HALF + PIECE), COPY)
-        nc.scalar.activation(*fetched(3, HALF + PIECE, S), COPY)
-        nc.scalar.copy(*placed(HALF, HALF + PIECE))
-        nc.scalar.copy(*placed(HALF + PIECE, S))
-        nc.vector.tensor_copy(*placed(0, PIECE))
-        nc.vector.tensor_copy(*placed(PIECE, HALF))
-        for lo in range(0, S, PIECE):
-            quantize(1, lo, lo + PIECE)
+        last = S - PIECE
+        nc.scalar.activation(picked[1][:, 0:last, 2], looked_up(1, 2, 0, last), COPY)
+        nc.vector.tensor_copy(last_pair[:, 0, :], looked_up(1, 2, last, S))
+        for lo in range(0, last, PIECE):
+            nc.scalar.activation(picked[1][:, lo : lo + PIECE, 3], looked_up(1, 3, lo, lo + PIECE), COPY)
+        nc.vector.tensor_copy(last_pair[:, 1, :], looked_up(1, 3, last, S))
+        quantize(1, 0, PIECE)
+        nc.vector.tensor_copy(picked[1][:, last:S, 2:PACK], last_pair[:].rearrange("p j s -> p s j"))
+        for piece in (1, 3, 2):
+            quantize(1, piece * PIECE, (piece + 1) * PIECE)
 
         results = [keep.tile([P, S], F32, name=f"results{b}") for b in range(BLOCKS)]
-        groups = ((0, 0, 128), (0, 128, 256), (1, 0, 256), (0, 256, 384), (0, 384, 512), (1, 256, 512))
-        acc = [psum.tile([P, hi - lo], F32, name=f"acc{b}_{lo}") for b, lo, hi in groups]
-        opened = set()
-        for g, z in ((0, 0), (2, 0), (3, 0), (4, 0), (5, 0), (0, 1), (1, 1), (2, 1), (1, 0), (3, 1), (4, 1), (5, 1)):
-            b, lo, hi = groups[g]
+        banks = ((0, 0, 1), (0, 1, 1), (0, 2, 1), (0, 3, 1), (1, 0, 2), (1, 2, 2))
+        acc = [psum.tile([P, n * PIECE], F32, name=f"acc{b}_{lo}") for b, lo, n in banks]
+        bank_of = {(b, lo + i): g for g, (b, lo, n) in enumerate(banks) for i in range(n)}
+        done = [0] * len(banks)
+        order = (
+            (0, 0, 0), (0, 1, 0), (0, 2, 0), (0, 3, 0), (1, 3, 0),
+            (0, 0, 1), (1, 0, 1), (1, 0, 0),
+            (0, 1, 1), (1, 1, 0),
+            (0, 3, 1), (1, 3, 1),
+            (0, 2, 1), (1, 1, 1), (1, 2, 0), (1, 2, 1),
+        )
+        for b, piece, z in order:
+            g = bank_of[b, piece]
+            first, n = banks[g][1], banks[g][2]
+            cols = slice(piece * PIECE, (piece + 1) * PIECE)
             nc.tensor.matmul_mx(
-                out=acc[g][:],
+                out=acc[g][:, (piece - first) * PIECE : (piece - first + 1) * PIECE],
                 lhsT=w_codes[z][:, b * P : (b + 1) * P].bitcast(FP8X4),
                 lhsT_scale=w_scales[:, z, b * P : (b + 1) * P],
-                rhs=x_codes[z][:, lo:hi].bitcast(FP8X4),
-                rhs_scale=x_scales[z][:, lo:hi],
-                start=(g not in opened),
-                stop=(g in opened),
+                rhs=x_codes[z][:, cols].bitcast(FP8X4),
+                rhs_scale=x_scales[z][:, cols],
+                start=(done[g] == 0),
+                stop=(done[g] == PASSES * n - 1),
             )
-            if g in opened:
-                nc.scalar.activation(results[b][:, lo:hi], acc[g][:], TANH)
-            opened.add(g)
+            done[g] = done[g] + 1
+            if done[g] == PASSES * n:
+                nc.scalar.activation(results[b][:, first * PIECE : (first + n) * PIECE], acc[g][:], TANH)
 
         for lo, hi in ((0, PIECE), (PIECE, S)):
             nc.vector.tensor_copy(window[0][:].indirect(entries(slot_sb, lo, hi)), results[0][:, lo:hi])
         nc.sync.dma_start(out[0:P, :], window[0][:])
-        for lo, hi in ((0, HALF), (HALF, S)):
-            nc.scalar.activation(window[1][:].indirect(entries(slot_sb, lo, hi)), results[1][:, lo:hi], COPY)
+        nc.scalar.activation(window[1][:].indirect(slot_sb[:]), results[1][:], COPY, scale=ones[:])
         nc.sync.dma_start(out[P : 2 * P, :], window[1][:])

@@ -105,16 +105,16 @@ def tile_picked_kvput_tanh_e_kernel(tc, xT, mem, w1_words, w1_scales, offs, slot
             quantize(1, piece * PIECE, (piece + 1) * PIECE)
 
         results = [keep.tile([P, S], F32, name=f"results{b}") for b in range(BLOCKS)]
-        banks = ((0, 0, 1), (0, 1, 1), (0, 2, 1), (0, 3, 1), (1, 0, 2), (1, 2, 2))
+        banks = tuple((b, piece, 1) for b in range(BLOCKS) for piece in range(S // PIECE))
         acc = [psum.tile([P, n * PIECE], F32, name=f"acc{b}_{lo}") for b, lo, n in banks]
         bank_of = {(b, lo + i): g for g, (b, lo, n) in enumerate(banks) for i in range(n)}
         done = [0] * len(banks)
         order = (
             (0, 0, 0), (0, 1, 0), (0, 2, 0), (0, 3, 0), (1, 3, 0),
             (0, 0, 1), (1, 0, 1), (1, 0, 0),
-            (0, 1, 1), (1, 1, 0),
-            (0, 3, 1), (1, 3, 1),
-            (0, 2, 1), (1, 1, 1), (1, 2, 0), (1, 2, 1),
+            (0, 1, 1), (1, 1, 1),
+            (0, 3, 1), (1, 1, 0),
+            (0, 2, 1), (1, 3, 1), (1, 2, 1), (1, 2, 0),
         )
         for b, piece, z in order:
             g = bank_of[b, piece]

@@ -71,7 +71,7 @@ def tile_picked_kvput_tanh_e_kernel(tc, xT, mem, w1_words, w1_scales, offs, slot
         x_codes = [keep.tile([P, S], U32, name=f"x_codes{z}", align_bytes=64) for z in range(PASSES)]
         x_scales = [keep.tile([P, S], U8, name=f"x_scales{z}", align_bytes=64) for z in range(PASSES)]
         dense = [keep.tile([P, PACK // (z + 1), HALF], F32, name=f"dense{z}") for z in range(PASSES)]
-        last_pair = keep.tile([P, 2, PIECE], BF16, name="last_pair")
+        last_pair = keep.tile([P, 2, 64], BF16, name="last_pair")
 
         def quantize(z, lo, hi):
             nc.vector.quantize_mx(
@@ -93,15 +93,15 @@ def tile_picked_kvput_tanh_e_kernel(tc, xT, mem, w1_words, w1_scales, offs, slot
             gather(1, j)
         nc.scalar.copy(picked[1][:, HALF:S, 0:2], dense[1][:].rearrange("p j s -> p s j"))
 
-        last = S - PIECE
-        nc.scalar.activation(picked[1][:, 0:last, 2], looked_up(1, 2, 0, last), COPY)
-        nc.vector.tensor_copy(last_pair[:, 0, :], looked_up(1, 2, last, S))
-        for lo in range(0, last, PIECE):
-            nc.scalar.activation(picked[1][:, lo : lo + PIECE, 3], looked_up(1, 3, lo, lo + PIECE), COPY)
-        nc.vector.tensor_copy(last_pair[:, 1, :], looked_up(1, 3, last, S))
-        quantize(1, 0, PIECE)
-        nc.vector.tensor_copy(picked[1][:, last:S, 2:PACK], last_pair[:].rearrange("p j s -> p s j"))
-        for piece in (1, 3, 2):
+        own_lo, own_hi = 448, 512
+        for lo, hi in ((0, own_lo),):
+            nc.scalar.activation(picked[1][:, lo:hi, 2], looked_up(1, 2, lo, hi), COPY)
+        nc.vector.tensor_copy(last_pair[:, 0, :], looked_up(1, 2, own_lo, own_hi))
+        for lo, hi in ((0, 128), (128, 256), (256, 384), (384, 448)):
+            nc.scalar.activation(picked[1][:, lo:hi, 3], looked_up(1, 3, lo, hi), COPY)
+        nc.vector.tensor_copy(last_pair[:, 1, :], looked_up(1, 3, own_lo, own_hi))
+        nc.vector.tensor_copy(picked[1][:, own_lo:own_hi, 2:PACK], last_pair[:].rearrange("p j s -> p s j"))
+        for piece in range(S // PIECE):
             quantize(1, piece * PIECE, (piece + 1) * PIECE)
 
         results = [keep.tile([P, S], F32, name=f"results{b}") for b in range(BLOCKS)]
@@ -112,9 +112,9 @@ def tile_picked_kvput_tanh_e_kernel(tc, xT, mem, w1_words, w1_scales, offs, slot
         order = (
             (0, 0, 0), (0, 1, 0), (0, 2, 0), (0, 3, 0), (1, 3, 0),
             (0, 0, 1), (1, 0, 1), (1, 0, 0),
-            (0, 1, 1), (1, 1, 1),
-            (0, 3, 1), (1, 1, 0),
-            (0, 2, 1), (1, 3, 1), (1, 2, 1), (1, 2, 0),
+            (0, 1, 1), (1, 1, 1), (1, 1, 0),
+            (0, 2, 1), (1, 2, 1), (1, 2, 0),
+            (0, 3, 1), (1, 3, 1),
         )
         for b, piece, z in order:
             g = bank_of[b, piece]

@@ -71,7 +71,7 @@ def tile_picked_kvput_tanh_e_kernel(tc, xT, mem, w1_words, w1_scales, offs, slot
         x_codes = [keep.tile([P, S], U32, name=f"x_codes{z}", align_bytes=64) for z in range(PASSES)]
         x_scales = [keep.tile([P, S], U8, name=f"x_scales{z}", align_bytes=64) for z in range(PASSES)]
         dense = [keep.tile([P, PACK // (z + 1), HALF], F32, name=f"dense{z}") for z in range(PASSES)]
-        last_pair = keep.tile([P, 2, 64], BF16, name="last_pair")
+        last_pair = keep.tile([P, 2, 96], BF16, name="last_pair")
 
         def quantize(z, lo, hi):
             nc.vector.quantize_mx(
@@ -93,11 +93,11 @@ def tile_picked_kvput_tanh_e_kernel(tc, xT, mem, w1_words, w1_scales, offs, slot
             gather(1, j)
         nc.scalar.copy(picked[1][:, HALF:S, 0:2], dense[1][:].rearrange("p j s -> p s j"))
 
-        own_lo, own_hi = 448, 512
-        for lo, hi in ((0, own_lo),):
+        own_lo, own_hi = 352, 448
+        for lo, hi in ((0, own_lo), (own_hi, S)):
             nc.scalar.activation(picked[1][:, lo:hi, 2], looked_up(1, 2, lo, hi), COPY)
         nc.vector.tensor_copy(last_pair[:, 0, :], looked_up(1, 2, own_lo, own_hi))
-        for lo, hi in ((0, 128), (128, 256), (256, 384), (384, 448)):
+        for lo, hi in ((0, 128), (128, 256), (256, 352), (448, 512)):
             nc.scalar.activation(picked[1][:, lo:hi, 3], looked_up(1, 3, lo, hi), COPY)
         nc.vector.tensor_copy(last_pair[:, 1, :], looked_up(1, 3, own_lo, own_hi))
         nc.vector.tensor_copy(picked[1][:, own_lo:own_hi, 2:PACK], last_pair[:].rearrange("p j s -> p s j"))
@@ -113,8 +113,8 @@ def tile_picked_kvput_tanh_e_kernel(tc, xT, mem, w1_words, w1_scales, offs, slot
             (0, 0, 0), (0, 1, 0), (0, 2, 0), (0, 3, 0), (1, 3, 0),
             (0, 0, 1), (1, 0, 1), (1, 0, 0),
             (0, 1, 1), (1, 1, 1), (1, 1, 0),
-            (0, 2, 1), (1, 2, 1), (1, 2, 0),
-            (0, 3, 1), (1, 3, 1),
+            (0, 2, 1), (1, 2, 1),
+            (0, 3, 1), (1, 2, 0), (1, 3, 1),
         )
         for b, piece, z in order:
             g = bank_of[b, piece]

from contextlib import ExitStack

import concourse.mybir as mybir

K, T, S, N, U = 1024, 2048, 512, 256, 1024
FLOPS = 2 * K * N * S

F32 = mybir.dt.float32
BF16 = mybir.dt.bfloat16
I32 = mybir.dt.int32
U32 = mybir.dt.uint32
U16 = mybir.dt.uint16
U8 = mybir.dt.uint8
FP8X4 = mybir.dt.float8_e4m3fn_x4
TANH = mybir.ActivationFunctionType.Tanh
COPY = mybir.ActivationFunctionType.Copy

P = 128
PACK = 4
PASSES = K // (P * PACK)
BLOCKS = N // P
LANES = 16
HALF = S // 2
PIECE = 128
LOADS = ((0, 0, 4), (1, 0, 2), (1, 2, 3), (1, 3, 4))


def tile_picked_kvput_tanh_e_kernel(tc, xT, mem, w1_words, w1_scales, offs, slot, out):
    nc = tc.nc
    with ExitStack() as ctx:
        keep = ctx.enter_context(tc.tile_pool(name="keep", bufs=1))
        psum = ctx.enter_context(tc.psum_pool(name="psum", bufs=1))

        offs_sb = keep.tile([P, S // LANES], U16, name="offs_sb")
        slot_sb = keep.tile([P, S // LANES], U16, name="slot_sb")
        w_codes = [keep.tile([P, N], U32, name=f"w_codes{z}", align_bytes=64) for z in range(PASSES)]
        w_scales = keep.tile([P, PASSES, N], U8, name="w_scales", align_bytes=64)
        slabs = [keep.tile([P, hi - lo, T], F32, name=f"slab{z}{lo}") for z, lo, hi in LOADS]
        plane = {(z, j): slab[:, j - lo, :] for slab, (z, lo, hi) in zip(slabs, LOADS) for j in range(lo, hi)}
        window = [keep.tile([P, U], F32, name=f"window{b}") for b in range(BLOCKS)]
        ones = keep.tile([P, 1], F32, name="ones")

        staged = keep.tile([P, PASSES, N], U8, name="staged")
        nc.gpsimd.memset(w_scales[:].rearrange("p z n -> p (z n)").bitcast(I32), 0)
        for q in range(4):
            live = slice(32 * q, 32 * q + 4)
            nc.scalar.dma_start(
                staged[live].bitcast(I32),
                w1_scales[:, 4 * q : 4 * q + 4, :].rearrange("z r n -> r z n").bitcast(I32),
            )
            nc.gpsimd.tensor_copy(w_scales[live].bitcast(I32), staged[live].bitcast(I32))
        nc.vector.memset(ones[:], 1.0)
        x_rows = xT.rearrange("(z p j) t -> z p j t", z=PASSES, j=PACK)
        for n, (z, lo, hi) in enumerate(LOADS):
            nc.sync.dma_start(slabs[n][:], x_rows[z, :, lo:hi, :])
            if n == 0:
                nc.sync.dma_start(offs_sb[:], offs)
        for z in range(PASSES):
            nc.sync.dma_start(w_codes[z][:].bitcast(I32), w1_words[z].rearrange("p n r -> p (n r)").bitcast(I32))
        nc.sync.dma_start(slot_sb[:], slot)
        for b in range(BLOCKS):
            nc.sync.dma_start(window[b][:], mem[b * P : (b + 1) * P, :])

        def entries(list_tile, lo, hi):
            return list_tile[:, lo // LANES : hi // LANES]

        def looked_up(z, j, lo, hi):
            return plane[z, j].indirect(entries(offs_sb, lo, hi))

        picked = [keep.tile([P, S, PACK], BF16, name=f"picked{z}", align_bytes=64) for z in range(PASSES)]
        x_codes = [keep.tile([P, S], U32, name=f"x_codes{z}", align_bytes=64) for z in range(PASSES)]
        x_scales = [keep.tile([P, S], U8, name=f"x_scales{z}", align_bytes=64) for z in range(PASSES)]
        dense = [keep.tile([P, PACK // (z + 1), HALF], F32, name=f"dense{z}") for z in range(PASSES)]
        last_pair = keep.tile([P, 2, 96], BF16, name="last_pair")

        def quantize(z, lo, hi):
            nc.vector.quantize_mx(
                out=x_codes[z][:, lo:hi].bitcast(FP8X4),
                scales=x_scales[z][:, lo:hi],
                in_=picked[z][:, lo:hi, :].rearrange("p s j -> p (s j)"),
            )

        def gather(z, j):
            nc.vector.tensor_copy(picked[z][:, 0:HALF, j], looked_up(z, j, 0, HALF))
            nc.scalar.activation(dense[z][:, j, :], looked_up(z, j, HALF, S), COPY)

        for j in range(PACK):
            gather(0, j)
        quantize(0, 0, HALF)
        nc.vector.tensor_copy(picked[0][:, HALF:S, :], dense[0][:].rearrange("p j s -> p s j"))
        quantize(0, HALF, S)
        for j in range(2):
            gather(1, j)
        nc.scalar.copy(picked[1][:, HALF:S, 0:2], dense[1][:].rearrange("p j s -> p s j"))

        own_lo, own_hi = 352, 448
        for lo, hi in ((0, own_lo), (own_hi, S)):
            nc.scalar.activation(picked[1][:, lo:hi, 2], looked_up(1, 2, lo, hi), COPY)
        nc.vector.tensor_copy(last_pair[:, 0, :], looked_up(1, 2, own_lo, own_hi))
        for lo, hi in ((0, 128), (128, 256), (256, 352), (448, 512)):
            nc.scalar.activation(picked[1][:, lo:hi, 3], looked_up(1, 3, lo, hi), COPY)
        nc.vector.tensor_copy(last_pair[:, 1, :], looked_up(1, 3, own_lo, own_hi))
        nc.vector.tensor_copy(picked[1][:, own_lo:own_hi, 2:PACK], last_pair[:].rearrange("p j s -> p s j"))
        for piece in range(S // PIECE):
            quantize(1, piece * PIECE, (piece + 1) * PIECE)

        results = [keep.tile([P, S], F32, name=f"results{b}") for b in range(BLOCKS)]
        banks = tuple((b, piece, 1) for b in range(BLOCKS) for piece in range(S // PIECE))
        acc = [psum.tile([P, n * PIECE], F32, name=f"acc{b}_{lo}") for b, lo, n in banks]
        bank_of = {(b, lo + i): g for g, (b, lo, n) in enumerate(banks) for i in range(n)}
        done = [0] * len(banks)
        order = (
            (0, 0, 0), (0, 1, 0), (0, 2, 0), (0, 3, 0), (1, 3, 0),
            (0, 0, 1), (1, 0, 1), (1, 0, 0),
            (0, 1, 1), (1, 1, 1), (1, 1, 0),
            (0, 2, 1), (1, 2, 1),
            (0, 3, 1), (1, 2, 0), (1, 3, 1),
        )
        for b, piece, z in order:
            g = bank_of[b, piece]
            first, n = banks[g][1], banks[g][2]
            cols = slice(piece * PIECE, (piece + 1) * PIECE)
            nc.tensor.matmul_mx(
                out=acc[g][:, (piece - first) * PIECE : (piece - first + 1) * PIECE],
                lhsT=w_codes[z][:, b * P : (b + 1) * P].bitcast(FP8X4),
                lhsT_scale=w_scales[:, z, b * P : (b + 1) * P],
                rhs=x_codes[z][:, cols].bitcast(FP8X4),
                rhs_scale=x_scales[z][:, cols],
                start=(done[g] == 0),
                stop=(done[g] == PASSES * n - 1),
            )
            done[g] = done[g] + 1
            if done[g] == PASSES * n:
                nc.scalar.activation(results[b][:, first * PIECE : (first + n) * PIECE], acc[g][:], TANH)

        for lo, hi in ((0, PIECE), (PIECE, S)):
            nc.vector.tensor_copy(window[0][:].indirect(entries(slot_sb, lo, hi)), results[0][:, lo:hi])
        nc.sync.dma_start(out[0:P, :], window[0][:])
        nc.scalar.activation(window[1][:].indirect(slot_sb[:]), results[1][:], COPY, scale=ones[:])
        nc.sync.dma_start(out[P : 2 * P, :], window[1][:])
